import numpy as np, ml_dtypes
CORES = [19,147,275,403]
N = 4
import mx_ref
NC, G = 128, 2
C = np.float32(0.041)
BF = ml_dtypes.bfloat16
def cut(t, i, w=512):
    return t[:, w * i:w * i + w]
def tile(rs):
    return np.stack(rs, axis=2).reshape(128, -1).astype(BF)
def layer(w, X):
    out = []
    for i in range(G):
        for t in range(len(X)):
            p = mx_ref.matmul(mx_ref.quantize(cut(w, len(X) * i + t)), X[t])
            z = p if t == 0 else z + p
        out.append(z)
    return out
def masked(A, E):
    return [(e * (s * a > 0)) * C for a, e in zip(A, E) for s in (1, -1)]
def setup_inputs(rng):
    def f(*shape):
        return mx_ref.flush((rng.standard_normal(shape, dtype=np.float32) * np.exp2(rng.integers(-2, 3, shape[:-1] + (1,)))).astype(BF))
    return {"x": f(N, 128, 512), "e": f(N, 128, 512), "a": f(N, 128, G * 512), "v": f(N, 128, 4 * NC)}
def setup_inputs_blocks(rng):
    d = setup_inputs(rng)
    for k in ("x", "e", "a", "v"): d[k] = mx_ref.spread(d[k], rng, 4)
    return d
def setup_inputs_wide(rng):
    d = setup_inputs(rng)
    for k in ("x", "e", "a", "v"): d[k] = mx_ref.flush((d[k].astype(np.float32) * np.exp2(rng.integers(-6, 7, (N, 1, 1))).astype(np.float32)).astype(BF))
    return d
def setup_inputs_zeros(rng):
    d = setup_inputs(rng); v = d["x"].reshape(N, 128, -1, 4).copy()
    v[np.broadcast_to((rng.random((N, 1, v.shape[2], 1)) < 0.33), v.shape)] = 0
    d["x"] = v.reshape(d["x"].shape)
    return d
def reference(x, e, a, v):
    T = [mx_ref.quantize(tile(masked(layer(a[j], [mx_ref.quantize(x[j])]), layer(a[j], [mx_ref.quantize(e[j])])))) for j in range(N)]
    y = np.zeros((N, 128, N * NC), np.float32)
    for r in range(N):
        qv = mx_ref.quantize(v[r])
        for j in range(N):
            y[r][:, NC * j:NC * j + NC] = mx_ref.matmul(T[j], qv)
    return {"y": y}

from concourse.mybir import dt, AluOpType, ActivationFunctionType

C = 0.041
W = 128

_CODES = "float8_e4m3fn_x4"
SCRATCH = {
    "xb": ("sbuf", [128, 4 * W], "bfloat16"),
    "eb": ("sbuf", [128, 4 * W], "bfloat16"),
    "vb": ("sbuf", [128, 4 * W], "bfloat16"),
    "ab": ("sbuf", [128, 8 * W], "bfloat16"),
    "xq": ("sbuf", [128, W], _CODES), "xs": ("sbuf", [128, W], "uint8"),
    "eq": ("sbuf", [128, W], _CODES), "es": ("sbuf", [128, W], "uint8"),
    "vq": ("sbuf", [128, W], _CODES), "vs": ("sbuf", [128, W], "uint8"),
    "aq": ("sbuf", [128, 2 * W], _CODES), "asc": ("sbuf", [128, 2 * W], "uint8"),
    "sg": ("sbuf", [128, 2 * W], "float32"),
    "mp": ("sbuf", [128, 2 * W], "float32"),
    "mn": ("sbuf", [128, 2 * W], "float32"),
    "h": ("sbuf", [128, 4 * W], "bfloat16"),
    "tq": ("sbuf", [128, W], _CODES), "ts": ("sbuf", [128, W], "uint8"),
    "cP": ("sbuf", [128, W], _CODES), "sP": ("sbuf", [128, W], "uint8"),
    "cN": ("sbuf", [128, W], _CODES), "sN": ("sbuf", [128, W], "uint8"),
    "cD": ("sbuf", [128, W], _CODES), "sD": ("sbuf", [128, W], "uint8"),
    "ysb": ("sbuf", [128, 4 * W], "float32"),
    "pU0": ("psum", [128, 512], "float32"), "pU1": ("psum", [128, 512], "float32"),
    "pD0": ("psum", [128, 512], "float32"), "pD1": ("psum", [128, 512], "float32"),
    "pY0": ("psum", [128, 512], "float32"), "pY1": ("psum", [128, 512], "float32"),
    "pY2": ("psum", [128, 512], "float32"), "pY3": ("psum", [128, 512], "float32"),
}
SEMAPHORES = [
    "lx", "la", "le", "lv",
    "qx", "qa0", "qa1", "qe", "qt", "qv",
    "mU0", "mU1", "mD0", "mD1",
    "sg0", "sg1", "mp0", "mn0", "mp1", "mn1",
    "pr",
    "aPc", "aPs", "aN", "aD",
    "sentA", "sentF",
    "mY0", "mY1", "mY2", "mY3",
    "cpE", "cpD",
    "st",
]


def _ring(T, topo):
    cores = list(T.cores)
    ring = [0]
    while len(ring) < len(cores):
        here = cores[ring[-1]]
        ring.append([q for q in range(len(cores)) if q not in ring and topo.may_write(here, cores[q])][0])
    return ring


def rank_program(g, core, T, topo):
    rank = T.rank_of(core)
    if rank is None:
        return
    S = T.sem
    ring = _ring(T, topo)
    n = len(ring)
    pos = ring.index(rank)
    nxt, prv, opp = ring[(pos + 1) % n], ring[(pos - 1) % n], ring[(pos + 2) % n]
    Act = ActivationFunctionType

    g.sync.dma_start(T.xb[:], T.x[:]).then_inc(S.lx, 16)
    g.scalar.dma_start(T.ab[:], T.a[:]).then_inc(S.la, 16)
    g.sync.dma_start(T.eb[:], T.e[:]).then_inc(S.le, 16)
    g.sync.dma_start(T.vb[:], T.v[:]).then_inc(S.lv, 16)

    v = g.vector
    v.wait_ge(S.lx, 16)
    v.quantize_mx(T.xq[:], T.xs[:], T.xb[:]).then_inc(S.qx, 1)
    v.wait_ge(S.la, 16)
    v.quantize_mx(T.aq[:, 0:W], T.asc[:, 0:W], T.ab[:, 0:4 * W]).then_inc(S.qa0, 1)
    v.quantize_mx(T.aq[:, W:2 * W], T.asc[:, W:2 * W], T.ab[:, 4 * W:8 * W]).then_inc(S.qa1, 1)
    v.wait_ge(S.le, 16)
    v.quantize_mx(T.eq[:], T.es[:], T.eb[:]).then_inc(S.qe, 1)

    t = g.tensor
    t.wait_ge(S.qx, 1)
    t.wait_ge(S.qa0, 1)
    t.matmul_mx(T.pU0[:, 0:W], T.aq[:, 0:W], T.asc[:, 0:W], T.xq[:], T.xs[:], True, True).then_inc(S.mU0, 1)
    t.wait_ge(S.qa1, 1)
    t.matmul_mx(T.pU1[:, 0:W], T.aq[:, W:2 * W], T.asc[:, W:2 * W], T.xq[:], T.xs[:], True, True).then_inc(S.mU1, 1)
    t.wait_ge(S.qe, 1)
    t.matmul_mx(T.pD0[:, 0:W], T.aq[:, 0:W], T.asc[:, 0:W], T.eq[:], T.es[:], True, True).then_inc(S.mD0, 1)
    t.matmul_mx(T.pD1[:, 0:W], T.aq[:, W:2 * W], T.asc[:, W:2 * W], T.eq[:], T.es[:], True, True).then_inc(S.mD1, 1)

    a = g.scalar
    for i, pU in enumerate((T.pU0, T.pU1)):
        cols = slice(W * i, W * i + W)
        a.wait_ge(S["mU%d" % i], 1)
        a.activation(T.sg[:, cols], pU[:, 0:W], Act.Sign).then_inc(S["sg%d" % i], 1)
        a.wait_ge(S["sg%d" % i], 1)
        a.activation(T.mp[:, cols], T.sg[:, cols], Act.Relu, scale=C).then_inc(S["mp%d" % i], 1)
        a.activation(T.mn[:, cols], T.sg[:, cols], Act.Relu, scale=-C).then_inc(S["mn%d" % i], 1)

    for i, pD in enumerate((T.pD0, T.pD1)):
        cols = slice(W * i, W * i + W)
        v.wait_ge(S["mD%d" % i], 1)
        v.wait_ge(S["mp%d" % i], 1)
        v.tensor_tensor(T.h[:, 2 * i:4 * W:4], pD[:, 0:W], T.mp[:, cols], AluOpType.mult).then_inc(S.pr, 1)
        v.wait_ge(S["mn%d" % i], 1)
        v.tensor_tensor(T.h[:, 2 * i + 1:4 * W:4], pD[:, 0:W], T.mn[:, cols], AluOpType.mult).then_inc(S.pr, 1)
    v.wait_ge(S.pr, 4)
    v.quantize_mx(T.tq[:], T.ts[:], T.h[:]).then_inc(S.qt, 1)
    v.wait_ge(S.lv, 16)
    v.quantize_mx(T.vq[:], T.vs[:], T.vb[:]).then_inc(S.qv, 1)

    def send(to_rank, out_ap, in_ap, remote_sem, local_sem):
        dst = T.cores[to_rank]
        rid, pid = topo.addr(dst, core)
        mask = topo.mask(core, dst)
        g.remote_dma(out_ap=out_ap, in_ap=in_ap, remote_sem=remote_sem, local_sem=local_sem,
                     pid=pid, routing_id=rid, dma_engine_mask=mask)
        return bin(mask).count("1")

    def engines(frm_rank):
        return bin(topo.mask(T.cores[frm_rank], core)).count("1")

    u8 = dt.uint8
    g.wait_ge(S.qt, 1)
    left = send(nxt, T.cP[:].bitcast(u8), T.tq[:].bitcast(u8), S.aPc, S.sentA)
    left += send(nxt, T.sP[:], T.ts[:], S.aPs, S.sentA)
    left += send(prv, T.cN[:].bitcast(u8), T.tq[:].bitcast(u8), S.aN, S.sentA)
    left += send(prv, T.sN[:], T.ts[:], S.aN, S.sentA)
    g.wait_ge(S.aPc, engines(prv))
    passed = send(nxt, T.cD[:].bitcast(u8), T.cP[:].bitcast(u8), S.aD, S.sentF)
    g.wait_ge(S.aPs, engines(prv))
    passed += send(nxt, T.sD[:], T.sP[:], S.aD, S.sentF)
    g.wait_ge(S.sentA, left)

    t.wait_ge(S.qt, 1)
    t.wait_ge(S.qv, 1)
    t.matmul_mx(T.pY0[:, 0:W], T.tq[:], T.ts[:], T.vq[:], T.vs[:], True, True).then_inc(S.mY0, 1)
    t.wait_ge(S.aPc, engines(prv))
    t.wait_ge(S.aPs, engines(prv))
    t.matmul_mx(T.pY1[:, 0:W], T.cP[:], T.sP[:], T.vq[:], T.vs[:], True, True).then_inc(S.mY1, 1)
    t.wait_ge(S.aN, 2 * engines(nxt))
    t.matmul_mx(T.pY2[:, 0:W], T.cN[:], T.sN[:], T.vq[:], T.vs[:], True, True).then_inc(S.mY2, 1)
    t.wait_ge(S.aD, 2 * engines(prv))
    t.matmul_mx(T.pY3[:, 0:W], T.cD[:], T.sD[:], T.vq[:], T.vs[:], True, True).then_inc(S.mY3, 1)

    def block(j):
        return slice(W * j, W * j + W)

    for k, (j, pY) in enumerate(((rank, T.pY0), (prv, T.pY1), (nxt, T.pY2), (opp, T.pY3))):
        v.wait_ge(S["mY%d" % k], 1)
        v.tensor_copy(T.ysb[:, block(j)], pY[:, 0:W]).then_inc(S.cpE if j != opp else S.cpD, 1)

    early = sorted((rank, prv, nxt))
    runs = [[early[0], early[0]]]
    for j in early[1:]:
        if j == runs[-1][1] + 1:
            runs[-1][1] = j
        else:
            runs.append([j, j])
    s = g.sync
    s.wait_ge(S.cpE, 3)
    s.wait_ge(S.sentF, passed)
    for lo, hi in runs:
        s.dma_start(T.y[:, W * lo:W * hi + W], T.ysb[:, W * lo:W * hi + W]).then_inc(S.st, 16)
    s.wait_ge(S.cpD, 1)
    s.dma_start(T.y[:, block(opp)], T.ysb[:, block(opp)]).then_inc(S.st, 16)
    s.wait_ge(S.st, 16 * (len(runs) + 1))
